import numpy as np
import ml_dtypes


def mxq(x, axis, fmt="e4m3"):
    dtype, down = {"e4m3": (ml_dtypes.float8_e4m3fn, 7), "e5m2": (ml_dtypes.float8_e5m2, 14)}[fmt]
    v = np.moveaxis(np.asarray(x, np.float32).astype(ml_dtypes.bfloat16).astype(np.float64), axis, -1)
    blocks = v.reshape(v.shape[:-1] + (-1, 32))
    amax = np.abs(blocks).max(-1, keepdims=True)
    byte = np.maximum(np.where(amax > 0, np.frexp(amax)[1] - 1 + 127, 0) - down, 1)
    scale = np.exp2(byte - 127.0)
    codes = (blocks / scale).astype(np.float32).astype(dtype).astype(np.float64)
    return np.moveaxis((codes * scale).reshape(v.shape), -1, axis)


WIDE = False


def mx_kscale(k):
    if not WIDE:
        return np.ones(k)
    levels = np.array([30, -30])
    if k % 512:
        return np.exp2(np.random.permutation(np.resize(levels, k // 32))).repeat(32)
    a = np.empty((k // 512, 16))
    for p in range(k // 512):
        a[p, :8] = np.random.permutation(np.resize(levels, 8))
        for g in range(8):
            far = levels[np.abs(levels - a[p, g]) >= 10]
            a[p, g + 8] = far[np.random.randint(len(far))]
    return np.exp2(a.ravel()).repeat(32)


def f64(x):
    return np.asarray(x).astype(np.float64)


def striped(idx):
    return np.tile(np.asarray(idx).reshape(-1, 16).T, (8, 1)).astype(np.uint16)


def unstriped(offs):
    return offs[:16].T.reshape(-1).astype(np.int64)


E2M1 = np.array([0.0, 0.5, 1.0, 1.5, 2.0, 3.0, 4.0, 6.0, -0.0, -0.5, -1.0, -1.5, -2.0, -3.0, -4.0, -6.0])


def pack_weight(w, fmt):
    k, n = w.shape
    w = f64(np.asarray(w, np.float32).astype(ml_dtypes.bfloat16)).reshape(k // 32, 32, n)
    amax = np.abs(w).max(1)
    if fmt in ("e4m3", "e5m2"):
        byte = np.frexp(amax)[1] - 1 + 127 - (7 if fmt == "e4m3" else 14)
    else:
        mant, ex = np.frexp(amax / 6.0)
        byte = np.where(mant > 0.5, ex, ex - 1) + 127
    byte = np.clip(np.where(amax > 0, byte, 1), 1, 254)
    scaled = (w * np.exp2(127.0 - byte)[:, None, :]).reshape(k, n).astype(np.float32)
    by_word = np.ascontiguousarray(scaled.reshape(k // 512, 128, 4, n).transpose(0, 1, 3, 2))
    if fmt in ("e4m3", "e5m2"):
        words = by_word.astype(ml_dtypes.float8_e4m3fn if fmt == "e4m3" else ml_dtypes.float8_e5m2).view(np.uint8)
    else:
        c = by_word.astype(ml_dtypes.float4_e2m1fn).view(np.uint8) & 0xF
        words = (c[..., 0::2] | (c[..., 1::2] << 4)).reshape(k // 512, 128, 2 * n)
    return np.ascontiguousarray(words), np.ascontiguousarray(byte.astype(np.uint8).reshape(k // 512, 16, n))


def unpack_weight(words, scales, fmt):
    g, _, n = scales.shape
    words = np.ascontiguousarray(words).reshape(g, 128, n, -1)
    if fmt in ("e4m3", "e5m2"):
        vals = words.view(ml_dtypes.float8_e4m3fn if fmt == "e4m3" else ml_dtypes.float8_e5m2).astype(np.float64)
    else:
        nib = np.empty((g, 128, n, 4), np.uint8)
        nib[..., 0::2] = words & 0xF
        nib[..., 1::2] = words >> 4
        vals = E2M1[nib]
    vals = vals * np.repeat(np.exp2(scales.astype(np.float64) - 127.0), 8, axis=1)[..., None]
    return vals.transpose(0, 1, 3, 2).reshape(g * 512, n)


K, T, J, R, F, Z, G, N = 512, 512, 256, 512, 512, 1024, 32, 256


def setup_inputs():
    n = np.random.standard_normal
    idx = np.random.permutation(T)[:J]
    idx2 = np.random.permutation(T)[:J]
    idx3 = np.random.permutation(Z)[:J]
    fk = mx_kscale(K)
    fr = mx_kscale(R)
    ff = mx_kscale(F)
    wp = pack_weight(n((K, R)) * 1 / np.sqrt(K) * fk[:, None] * fr, "e4m3")
    xop = pack_weight(n((F, Z)) / ff[:, None], "e2m1")
    w2p = pack_weight(n((F, R)) * 1 / np.sqrt(F) * ff[:, None] * fr, "e5m2")
    wbp = pack_weight(n((R, N)) * 1 / np.sqrt(R) / fr[:, None], "e2m1")
    return {
        "xf": (n((K, T))).astype(np.float32),
        "fk": (np.random.uniform(0.5, 2.0, (K, 1)) / fk[:, None]).astype(np.float32),
        "w_words": wp[0],
        "w_scales": wp[1],
        "xo_words": xop[0],
        "xo_scales": xop[1],
        "w2_words": w2p[0],
        "w2_scales": w2p[1],
        "wb_words": wbp[0],
        "wb_scales": wbp[1],
        "bi": (np.random.uniform(-0.5, 0.5, (1, N))).astype(np.float32),
        "offs": striped(idx),
        "offs2": striped(idx2),
        "offs3": striped(idx3),
    }


def reference(xf, fk, w_words, w_scales, xo_words, xo_scales, w2_words, w2_scales, wb_words, wb_scales, bi, offs, offs2, offs3):
    idx = unstriped(offs)
    idx2 = unstriped(offs2)
    idx3 = unstriped(offs3)
    wu = unpack_weight(w_words, w_scales, "e4m3")
    xou = unpack_weight(xo_words, xo_scales, "e2m1")
    w2u = unpack_weight(w2_words, w2_scales, "e5m2")
    wbu = unpack_weight(wb_words, wb_scales, "e2m1")
    u = np.maximum(f64(xf)[:, idx], f64(xf)[:, idx2]) * f64(fk)
    uq = mxq(u, 0, "e4m3")
    xoidx3g = xou[:, idx3]
    a = wu.T @ uq + w2u.T @ xoidx3g
    m1 = a.reshape(R, G, J // G).mean(axis=2)
    m2 = np.repeat(m1, J // G, axis=1)
    hid = a - m2
    hidq = mxq(hid, 0, "e5m2")
    p = hidq.T @ wbu
    ea = np.exp(0.7 * p + f64(bi))
    y = 256.0 * ea / np.sum(ea, axis=1, keepdims=True)
    return y

@@ -1,0 +1,235 @@
+from contextlib import ExitStack
+
+import concourse.mybir as mybir
+
+K, T, J, R, F, Z, G, N = 512, 512, 256, 512, 512, 1024, 32, 256
+FLOPS = 2 * K * R * J + 2 * F * R * J + 2 * R * J * N
+
+F32 = mybir.dt.float32
+BF16 = mybir.dt.bfloat16
+I32 = mybir.dt.int32
+U32 = mybir.dt.uint32
+U16 = mybir.dt.uint16
+U8 = mybir.dt.uint8
+E4M3 = mybir.dt.float8_e4m3fn_x4
+E5M2 = mybir.dt.float8_e5m2_x4
+E2M1 = mybir.dt.float4_e2m1fn_x4
+ALU = mybir.AluOpType
+ACT = mybir.ActivationFunctionType
+AX = mybir.AxisListType
+
+P = 128
+PACK = 4
+HALF = 128
+BUNDLE = J // G
+LINE = 4
+
+
+def load_scale_rows(queue, plane, first_row, scales):
+    for q in range(4):
+        row = 32 * q + first_row
+        queue.dma_start(out=plane[row : row + 4, :].bitcast(I32), in_=scales[0, 4 * q : 4 * q + 4, :].bitcast(I32))
+
+
+def tile_list_sum_largerpicks_othertable_levelled_rowshares_kernel(
+    tc, xf, fk, w_words, w_scales, xo_words, xo_scales, w2_words, w2_scales, wb_words, wb_scales, bi, offs, offs2, offs3, out
+):
+    nc = tc.nc
+    with ExitStack() as ctx:
+        sb = ctx.enter_context(tc.tile_pool(name="sb", bufs=1))
+        ps = ctx.enter_context(tc.psum_pool(name="ps", bufs=1))
+
+        list1 = sb.tile([P, J // 16], U16, name="list1")
+        list2 = sb.tile([P, J // 16], U16, name="list2")
+        list3 = sb.tile([P, J // 16], U16, name="list3")
+        x_pair = [sb.tile([P, 2, T], F32, name=f"x_pair{a}", align_bytes=64) for a in range(2)]
+        factor = sb.tile([P, PACK], F32, name="factor")
+        bias = sb.tile([P, N], F32, name="bias")
+        xo_w = sb.tile([P, Z], U16, name="xo_w", align_bytes=64)
+        xo_s = sb.tile([P, Z], U8, name="xo_s", align_bytes=64)
+        w_raw = sb.tile([P, R], U32, name="w_raw", align_bytes=64)
+        w2_raw = sb.tile([P, R], U32, name="w2_raw", align_bytes=64)
+        ws_raw = sb.tile([P, R], U8, name="ws_raw", align_bytes=64)
+        wb_w = sb.tile([P, 2 * N], U8, name="wb_w", align_bytes=64)
+        wb_s = sb.tile([P, N], U8, name="wb_s", align_bytes=64)
+
+        nc.vector.memset(xo_s[:].bitcast(I32), 0)
+        nc.vector.memset(ws_raw[:].bitcast(I32), 0)
+        nc.vector.memset(wb_s[:].bitcast(I32), 0)
+
+        x_rows = xf.rearrange("(p t) c -> p t c", t=PACK)
+        nc.sync.dma_start(list1[:], offs)
+        nc.sync.dma_start(list2[:], offs2)
+        nc.sync.dma_start(out=x_pair[0][:], in_=x_rows[:, 0:2, :])
+        nc.sync.dma_start(out=x_pair[1][:], in_=x_rows[:, 2:4, :])
+        load_scale_rows(nc.scalar, xo_s, 0, xo_scales)
+        nc.sync.dma_start(list3[:], offs3)
+        nc.sync.dma_start(out=xo_w[:].bitcast(I32), in_=xo_words[0].bitcast(I32))
+        nc.sync.dma_start(out=factor[:], in_=fk.rearrange("(p t) o -> p (t o)", t=PACK))
+        nc.sync.dma_start(out=w2_raw[:].bitcast(I32), in_=w2_words[0].rearrange("p n t -> p (n t)").bitcast(I32))
+        nc.sync.dma_start(out=w_raw[:].bitcast(I32), in_=w_words[0].rearrange("p n t -> p (n t)").bitcast(I32))
+        load_scale_rows(nc.sync, ws_raw, 0, w2_scales)
+        load_scale_rows(nc.sync, ws_raw, 4, w_scales)
+        nc.sync.dma_start(out=wb_w[:].bitcast(I32), in_=wb_words[0].bitcast(I32))
+        load_scale_rows(nc.sync, wb_s, 0, wb_scales)
+        nc.sync.dma_start(out=bias[:], in_=bi[0].partition_broadcast(P))
+
+        pick1 = [sb.tile([P, 2, J], F32, name=f"pick1_{a}") for a in range(2)]
+        pick2 = [sb.tile([P, 2, J], F32, name=f"pick2_{a}") for a in range(2)]
+        larger = sb.tile([P, PACK, J], F32, name="larger")
+
+        for e in range(2):
+            nc.scalar.activation(pick1[0][:, e, :], x_pair[0][:, e, :].indirect(list1[:]), ACT.Copy)
+            nc.vector.tensor_copy(pick2[0][:, e, :], x_pair[0][:, e, :].indirect(list2[:]))
+        for e in range(2):
+            nc.scalar.activation(pick1[1][:, e, :], x_pair[1][:, e, :].indirect(list1[:]), ACT.Copy)
+            nc.scalar.activation(pick2[1][:, e, :], x_pair[1][:, e, :].indirect(list2[:]), ACT.Copy)
+        nc.vector.tensor_tensor(larger[:, 0:2, :], pick1[0][:], pick2[0][:], ALU.max)
+
+        xg_w = sb.tile([P, J], U16, name="xg_w", align_bytes=64)
+        xg_s = sb.tile([P, J], U8, name="xg_s", align_bytes=64)
+        nc.vector.tensor_copy(xg_w[:], xo_w[:].indirect(list3[:]))
+        nc.vector.tensor_copy(xg_s[:], xo_s[:].indirect(list3[:]))
+
+        w_dealt = sb.tile([P, PACK, P], U32, name="w_dealt", align_bytes=64)
+        w2_dealt = sb.tile([P, PACK, P], U32, name="w2_dealt", align_bytes=64)
+        ws_dealt = sb.tile([P, PACK, P], U8, name="ws_dealt", align_bytes=64)
+        for dealt, raw in ((w2_dealt, w2_raw), (w_dealt, w_raw)):
+            nc.vector.tensor_copy(
+                dealt[:].rearrange("p t (c i) -> p c t i", i=LINE),
+                raw[:].rearrange("p (c i t) -> p c t i", i=LINE, t=PACK),
+            )
+
+        nc.vector.tensor_tensor(larger[:, 2:4, :], pick1[1][:], pick2[1][:], ALU.max)
+
+        halves = range(J // HALF)
+        u_b = [sb.tile([P, HALF, PACK], BF16, name=f"u_b{h}", align_bytes=64) for h in halves]
+        u_w = [sb.tile([P, HALF], U32, name=f"u_w{h}", align_bytes=64) for h in halves]
+        u_s = [sb.tile([P, HALF], U8, name=f"u_s{h}", align_bytes=64) for h in halves]
+        hid_b = [sb.tile([P, HALF, PACK], BF16, name=f"hid_b{h}", align_bytes=64) for h in halves]
+        hid_w = [sb.tile([P, HALF], U32, name=f"hid_w{h}", align_bytes=64) for h in halves]
+        hid_s = [sb.tile([P, HALF], U8, name=f"hid_s{h}", align_bytes=64) for h in halves]
+        sums = [sb.tile([P, PACK, HALF // BUNDLE], F32, name=f"sums{h}") for h in halves]
+        means = [sb.tile([P, PACK, HALF // BUNDLE], F32, name=f"means{h}") for h in halves]
+        neg_z = [sb.tile([P, N], F32, name=f"neg_z{h}") for h in halves]
+        neg_max = [sb.tile([P, 1], F32, name=f"neg_max{h}") for h in halves]
+        ea = [sb.tile([P, N], F32, name=f"ea{h}") for h in halves]
+        total = [sb.tile([P, 1], F32, name=f"total{h}") for h in halves]
+        inv = [sb.tile([P, 1], F32, name=f"inv{h}") for h in halves]
+        y = [sb.tile([P, N], F32, name=f"y{h}") for h in halves]
+        a_ps = [ps.tile([P, PACK, HALF], F32, name=f"a_ps{h}") for h in halves]
+        p_ps = [ps.tile([P, N], F32, name=f"p_ps{h}") for h in halves]
+
+        def cols(h):
+            return slice(h * HALF, (h + 1) * HALF)
+
+        def scale_u(h):
+            nc.vector.tensor_tensor(
+                u_b[h][:].rearrange("p (c i) t -> p c t i", i=LINE),
+                larger[:, :, cols(h)].rearrange("p t (c i) -> p c t i", i=LINE),
+                factor[:].unsqueeze(1).unsqueeze(3).to_broadcast([P, HALF // LINE, PACK, LINE]),
+                ALU.mult,
+            )
+
+        def quantise(words, scales, values, fmt):
+            nc.vector.quantize_mx(out=words[:].bitcast(fmt), scales=scales[:], in_=values[:].rearrange("p j t -> p (j t)"))
+
+        def side_passes(h):
+            for t in range(PACK):
+                nc.tensor.matmul_mx(
+                    out=a_ps[h][:, t, :],
+                    lhsT=w2_dealt[:, t, :].bitcast(E5M2),
+                    lhsT_scale=ws_dealt[:, t, :],
+                    rhs=xg_w[:, cols(h)].bitcast(E2M1),
+                    rhs_scale=xg_s[:, cols(h)],
+                    start=(t == 0),
+                    stop=False,
+                )
+
+        def main_passes(h):
+            for t in range(PACK):
+                nc.tensor.matmul_mx(
+                    out=a_ps[h][:, t, :],
+                    lhsT=w_dealt[:, t, :].bitcast(E4M3),
+                    lhsT_scale=ws_dealt[4:P, t, :],
+                    rhs=u_w[h][:].bitcast(E4M3),
+                    rhs_scale=u_s[h][:],
+                    start=False,
+                    stop=(t == PACK - 1),
+                )
+
+        def bundle_sums(h):
+            nc.vector.tensor_reduce(
+                sums[h][:].rearrange("p t g -> p (t g)"),
+                a_ps[h][:].rearrange("p t (g i) -> p (t g) i", i=BUNDLE),
+                AX.X,
+                ALU.add,
+            )
+
+        def bundle_means(h):
+            nc.vector.tensor_scalar(means[h][:], sums[h][:], 1.0 / BUNDLE, None, ALU.mult)
+
+        def level(h):
+            nc.vector.tensor_tensor(
+                hid_b[h][:].rearrange("p (g i) t -> p g i t", i=BUNDLE),
+                a_ps[h][:].rearrange("p t (g i) -> p g i t", i=BUNDLE),
+                means[h][:].rearrange("p t g -> p g t").unsqueeze(2).to_broadcast([P, HALF // BUNDLE, BUNDLE, PACK]),
+                ALU.subtract,
+            )
+
+        def second_layer(h):
+            nc.tensor.matmul_mx(
+                out=p_ps[h][:],
+                lhsT=hid_w[h][:].bitcast(E5M2),
+                lhsT_scale=hid_s[h][:],
+                rhs=wb_w[:].bitcast(E2M1),
+                rhs_scale=wb_s[:],
+                start=True,
+                stop=True,
+            )
+
+        def logits(h):
+            nc.vector.scalar_tensor_tensor(neg_z[h][:], p_ps[h][:], -0.7, bias[:], ALU.mult, ALU.subtract)
+
+        def row_max(h):
+            nc.vector.tensor_reduce(neg_max[h][:], neg_z[h][:], AX.X, ALU.min)
+
+        def exponentials(h):
+            nc.scalar.activation(ea[h][:], neg_z[h][:], ACT.Exp, bias=neg_max[h][:], scale=-1.0, accum_out=total[h][:])
+
+        def invert(h):
+            nc.vector.reciprocal(inv[h][:], total[h][:])
+
+        def shares(h):
+            nc.vector.tensor_scalar(y[h][:], ea[h][:], inv[h][:], 256.0, ALU.mult, ALU.mult)
+            nc.sync.dma_start(out=out[cols(h), :], in_=y[h][:])
+
+        scale_u(0)
+        nc.vector.tensor_copy(ws_dealt[:], ws_raw[:].rearrange("p (m t) -> p t m", t=PACK))
+        side_passes(0)
+        side_passes(1)
+        quantise(u_w[0], u_s[0], u_b[0], E4M3)
+        main_passes(0)
+        scale_u(1)
+        bundle_sums(0)
+        quantise(u_w[1], u_s[1], u_b[1], E4M3)
+        main_passes(1)
+        bundle_means(0)
+        level(0)
+        bundle_sums(1)
+        quantise(hid_w[0], hid_s[0], hid_b[0], E5M2)
+        second_layer(0)
+        bundle_means(1)
+        level(1)
+        logits(0)
+        quantise(hid_w[1], hid_s[1], hid_b[1], E5M2)
+        second_layer(1)
+        row_max(0)
+        exponentials(0)
+        logits(1)
+        row_max(1)
+        exponentials(1)
+        invert(0)
+        shares(0)
+        invert(1)
+        shares(1)

@@ -25,8 +25,8 @@ BUNDLE = J // G
 LINE = 4
 
 
-def load_scale_rows(queue, plane, first_row, scales):
-    for q in range(4):
+def load_scale_rows(queue, plane, first_row, scales, quadrants):
+    for q in quadrants:
         row = 32 * q + first_row
         queue.dma_start(out=plane[row : row + 4, :].bitcast(I32), in_=scales[0, 4 * q : 4 * q + 4, :].bitcast(I32))
 
@@ -42,74 +42,100 @@ def tile_list_sum_largerpicks_othertable_levelled_rowshares_kernel(
         list1 = sb.tile([P, J // 16], U16, name="list1")
         list2 = sb.tile([P, J // 16], U16, name="list2")
         list3 = sb.tile([P, J // 16], U16, name="list3")
-        x_pair = [sb.tile([P, 2, T], F32, name=f"x_pair{a}", align_bytes=64) for a in range(2)]
+        x_pair = [sb.tile([P, 2, T], F32, name=f"x_pair{a}", tag=f"x_pair{a}", align_bytes=64) for a in range(2)]
         factor = sb.tile([P, PACK], F32, name="factor")
-        bias = sb.tile([P, N], F32, name="bias")
-        xo_w = sb.tile([P, Z], U16, name="xo_w", align_bytes=64)
+        xo_w = sb.tile([P, Z], U16, name="xo_w", tag="xo_w", align_bytes=64)
         xo_s = sb.tile([P, Z], U8, name="xo_s", align_bytes=64)
         w_raw = sb.tile([P, R], U32, name="w_raw", align_bytes=64)
         w2_raw = sb.tile([P, R], U32, name="w2_raw", align_bytes=64)
-        ws_raw = sb.tile([P, R], U8, name="ws_raw", align_bytes=64)
-        wb_w = sb.tile([P, 2 * N], U8, name="wb_w", align_bytes=64)
+        ws_raw = sb.tile([P, R], U8, name="ws_raw", tag="larger", align_bytes=64)
         wb_s = sb.tile([P, N], U8, name="wb_s", align_bytes=64)
 
         nc.vector.memset(xo_s[:].bitcast(I32), 0)
         nc.vector.memset(ws_raw[:].bitcast(I32), 0)
+        warm = sb.tile([P, 2], F32, name="warm")
+        nc.vector.memset(warm[:, 0:1], 0.0)
+        nc.scalar.activation(warm[:, 1:2], warm[:, 0:1], ACT.Exp)
         nc.vector.memset(wb_s[:].bitcast(I32), 0)
 
+        def load_words(tile, words):
+            nc.sync.dma_start(out=tile.bitcast(I32), in_=words.bitcast(I32))
+
         x_rows = xf.rearrange("(p t) c -> p t c", t=PACK)
+        load_scale_rows(nc.gpsimd, ws_raw, 0, w2_scales, range(1, 4))
         nc.sync.dma_start(list1[:], offs)
         nc.sync.dma_start(list2[:], offs2)
         nc.sync.dma_start(out=x_pair[0][:], in_=x_rows[:, 0:2, :])
-        nc.sync.dma_start(out=x_pair[1][:], in_=x_rows[:, 2:4, :])
-        load_scale_rows(nc.scalar, xo_s, 0, xo_scales)
         nc.sync.dma_start(list3[:], offs3)
-        nc.sync.dma_start(out=xo_w[:].bitcast(I32), in_=xo_words[0].bitcast(I32))
+        load_words(xo_w[:], xo_words[0])
+        load_scale_rows(nc.sync, xo_s, 0, xo_scales, range(4))
+        nc.sync.dma_start(out=x_pair[1][:], in_=x_rows[:, 2:4, :])
+        load_words(w2_raw[:], w2_words[0].rearrange("p n t -> p (n t)"))
+        load_words(w_raw[:], w_words[0].rearrange("p n t -> p (n t)"))
+        load_scale_rows(nc.sync, ws_raw, 4, w_scales, range(4))
+        load_scale_rows(nc.sync, ws_raw, 0, w2_scales, range(1))
         nc.sync.dma_start(out=factor[:], in_=fk.rearrange("(p t) o -> p (t o)", t=PACK))
-        nc.sync.dma_start(out=w2_raw[:].bitcast(I32), in_=w2_words[0].rearrange("p n t -> p (n t)").bitcast(I32))
-        nc.sync.dma_start(out=w_raw[:].bitcast(I32), in_=w_words[0].rearrange("p n t -> p (n t)").bitcast(I32))
-        load_scale_rows(nc.sync, ws_raw, 0, w2_scales)
-        load_scale_rows(nc.sync, ws_raw, 4, w_scales)
-        nc.sync.dma_start(out=wb_w[:].bitcast(I32), in_=wb_words[0].bitcast(I32))
-        load_scale_rows(nc.sync, wb_s, 0, wb_scales)
-        nc.sync.dma_start(out=bias[:], in_=bi[0].partition_broadcast(P))
+        load_scale_rows(nc.sync, wb_s, 0, wb_scales, range(4))
 
-        pick1 = [sb.tile([P, 2, J], F32, name=f"pick1_{a}") for a in range(2)]
-        pick2 = [sb.tile([P, 2, J], F32, name=f"pick2_{a}") for a in range(2)]
-        larger = sb.tile([P, PACK, J], F32, name="larger")
+        halves = range(J // HALF)
 
+        def cols(h):
+            return slice(h * HALF, (h + 1) * HALF)
+
+        def entries(h):
+            return slice(h * HALF // 16, (h + 1) * HALF // 16)
+
+        pick1 = sb.tile([P, PACK, J], F32, name="pick1")
+        pick2 = sb.tile([P, PACK, J], F32, name="pick2")
+        nc.vector.tensor_copy(pick2[:, 0, :], x_pair[0][:, 0, :].indirect(list2[:]))
         for e in range(2):
-            nc.scalar.activation(pick1[0][:, e, :], x_pair[0][:, e, :].indirect(list1[:]), ACT.Copy)
-            nc.vector.tensor_copy(pick2[0][:, e, :], x_pair[0][:, e, :].indirect(list2[:]))
-        for e in range(2):
-            nc.scalar.activation(pick1[1][:, e, :], x_pair[1][:, e, :].indirect(list1[:]), ACT.Copy)
-            nc.scalar.activation(pick2[1][:, e, :], x_pair[1][:, e, :].indirect(list2[:]), ACT.Copy)
-        nc.vector.tensor_tensor(larger[:, 0:2, :], pick1[0][:], pick2[0][:], ALU.max)
+            nc.scalar.activation(pick1[:, e, :], x_pair[0][:, e, :].indirect(list1[:]), ACT.Copy)
+        nc.scalar.activation(pick2[:, 1, :], x_pair[0][:, 1, :].indirect(list2[:]), ACT.Copy)
+        for h in halves:
+            for picked, entry_list in ((pick1, list1), (pick2, list2)):
+                for e in range(2):
+                    nc.scalar.activation(
+                        picked[:, 2 + e, cols(h)], x_pair[1][:, e, :].indirect(entry_list[:, entries(h)]), ACT.Copy
+                    )
+
+        wb_w = sb.tile([P, 2 * N], U8, name="wb_w", tag="x_pair0", align_bytes=64)
+        load_words(wb_w[:], wb_words[0])
 
         xg_w = sb.tile([P, J], U16, name="xg_w", align_bytes=64)
         xg_s = sb.tile([P, J], U8, name="xg_s", align_bytes=64)
-        nc.vector.tensor_copy(xg_w[:], xo_w[:].indirect(list3[:]))
         nc.vector.tensor_copy(xg_s[:], xo_s[:].indirect(list3[:]))
+        nc.vector.tensor_copy(xg_w[:], xo_w[:].indirect(list3[:]))
+        bias = sb.tile([P, N], F32, name="bias", tag="xo_w", align_bytes=64)
+        nc.sync.dma_start(out=bias[:], in_=bi[0].partition_broadcast(P))
 
         w_dealt = sb.tile([P, PACK, P], U32, name="w_dealt", align_bytes=64)
         w2_dealt = sb.tile([P, PACK, P], U32, name="w2_dealt", align_bytes=64)
         ws_dealt = sb.tile([P, PACK, P], U8, name="ws_dealt", align_bytes=64)
-        for dealt, raw in ((w2_dealt, w2_raw), (w_dealt, w_raw)):
+
+        def deal_words(dealt, raw):
             nc.vector.tensor_copy(
-                dealt[:].rearrange("p t (c i) -> p c t i", i=LINE),
-                raw[:].rearrange("p (c i t) -> p c t i", i=LINE, t=PACK),
+                dealt.rearrange("p t (c i) -> p c t i", i=LINE),
+                raw.rearrange("p (c i t) -> p c t i", i=LINE, t=PACK),
             )
 
-        nc.vector.tensor_tensor(larger[:, 2:4, :], pick1[1][:], pick2[1][:], ALU.max)
+        larger = []
 
-        halves = range(J // HALF)
-        u_b = [sb.tile([P, HALF, PACK], BF16, name=f"u_b{h}", align_bytes=64) for h in halves]
+        def keep_larger(h):
+            larger.append(sb.tile([P, PACK, HALF], F32, name=f"larger{h}", tag="larger", align_bytes=64))
+            nc.vector.tensor_tensor(larger[h][:], pick1[:, :, cols(h)], pick2[:, :, cols(h)], ALU.max)
+
+        deal_words(w2_dealt[:], w2_raw[:])
+        deal_words(w_dealt[:], w_raw[:])
+        nc.vector.tensor_copy(ws_dealt[:], ws_raw[:].rearrange("p (m t) -> p t m", t=PACK))
+        keep_larger(0)
+
+        u_b = [sb.tile([P, HALF, PACK], BF16, name="u_b0", align_bytes=64)]
         u_w = [sb.tile([P, HALF], U32, name=f"u_w{h}", align_bytes=64) for h in halves]
         u_s = [sb.tile([P, HALF], U8, name=f"u_s{h}", align_bytes=64) for h in halves]
         hid_b = [sb.tile([P, HALF, PACK], BF16, name=f"hid_b{h}", align_bytes=64) for h in halves]
         hid_w = [sb.tile([P, HALF], U32, name=f"hid_w{h}", align_bytes=64) for h in halves]
         hid_s = [sb.tile([P, HALF], U8, name=f"hid_s{h}", align_bytes=64) for h in halves]
-        sums = [sb.tile([P, PACK, HALF // BUNDLE], F32, name=f"sums{h}") for h in halves]
+        sums = []
         means = [sb.tile([P, PACK, HALF // BUNDLE], F32, name=f"means{h}") for h in halves]
         neg_z = [sb.tile([P, N], F32, name=f"neg_z{h}") for h in halves]
         neg_max = [sb.tile([P, 1], F32, name=f"neg_max{h}") for h in halves]
@@ -120,13 +146,10 @@ def tile_list_sum_largerpicks_othertable_levelled_rowshares_kernel(
         a_ps = [ps.tile([P, PACK, HALF], F32, name=f"a_ps{h}") for h in halves]
         p_ps = [ps.tile([P, N], F32, name=f"p_ps{h}") for h in halves]
 
-        def cols(h):
-            return slice(h * HALF, (h + 1) * HALF)
-
         def scale_u(h):
             nc.vector.tensor_tensor(
                 u_b[h][:].rearrange("p (c i) t -> p c t i", i=LINE),
-                larger[:, :, cols(h)].rearrange("p t (c i) -> p c t i", i=LINE),
+                larger[h][:].rearrange("p t (c i) -> p c t i", i=LINE),
                 factor[:].unsqueeze(1).unsqueeze(3).to_broadcast([P, HALF // LINE, PACK, LINE]),
                 ALU.mult,
             )
@@ -158,7 +181,8 @@ def tile_list_sum_largerpicks_othertable_levelled_rowshares_kernel(
                     stop=(t == PACK - 1),
                 )
 
-        def bundle_sums(h):
+        def bundle_sums(h, tag):
+            sums.append(sb.tile([P, PACK, HALF // BUNDLE], F32, name=f"sums{h}", tag=tag, align_bytes=64))
             nc.vector.tensor_reduce(
                 sums[h][:].rearrange("p t g -> p (t g)"),
                 a_ps[h][:].rearrange("p t (g i) -> p (t g) i", i=BUNDLE),
@@ -167,7 +191,7 @@ def tile_list_sum_largerpicks_othertable_levelled_rowshares_kernel(
             )
 
         def bundle_means(h):
-            nc.vector.tensor_scalar(means[h][:], sums[h][:], 1.0 / BUNDLE, None, ALU.mult)
+            nc.scalar.activation(means[h][:], sums[h][:], ACT.Copy, scale=1.0 / BUNDLE)
 
         def level(h):
             nc.vector.tensor_tensor(
@@ -204,32 +228,30 @@ def tile_list_sum_largerpicks_othertable_levelled_rowshares_kernel(
             nc.vector.tensor_scalar(y[h][:], ea[h][:], inv[h][:], 256.0, ALU.mult, ALU.mult)
             nc.sync.dma_start(out=out[cols(h), :], in_=y[h][:])
 
-        scale_u(0)
-        nc.vector.tensor_copy(ws_dealt[:], ws_raw[:].rearrange("p (m t) -> p t m", t=PACK))
         side_passes(0)
         side_passes(1)
+        scale_u(0)
+        keep_larger(1)
         quantise(u_w[0], u_s[0], u_b[0], E4M3)
         main_passes(0)
+        u_b.append(sb.tile([P, HALF, PACK], BF16, name="u_b1", tag="u_b1", align_bytes=64))
         scale_u(1)
-        bundle_sums(0)
         quantise(u_w[1], u_s[1], u_b[1], E4M3)
         main_passes(1)
+        bundle_sums(0, "u_b1")
         bundle_means(0)
-        level(0)
-        bundle_sums(1)
-        quantise(hid_w[0], hid_s[0], hid_b[0], E5M2)
-        second_layer(0)
+        bundle_sums(1, "sums1")
         bundle_means(1)
-        level(1)
-        logits(0)
-        quantise(hid_w[1], hid_s[1], hid_b[1], E5M2)
-        second_layer(1)
-        row_max(0)
-        exponentials(0)
-        logits(1)
-        row_max(1)
-        exponentials(1)
-        invert(0)
-        shares(0)
-        invert(1)
-        shares(1)
+        for h in halves:
+            level(h)
+        for h in halves:
+            quantise(hid_w[h], hid_s[h], hid_b[h], E5M2)
+            second_layer(h)
+        for h in halves:
+            logits(h)
+        for h in halves:
+            row_max(h)
+            exponentials(h)
+        for h in halves:
+            invert(h)
+            shares(h)

from contextlib import ExitStack

import concourse.mybir as mybir

K, T, J, R, F, Z, G, N = 512, 512, 256, 512, 512, 1024, 32, 256
FLOPS = 2 * K * R * J + 2 * F * R * J + 2 * R * J * N

F32 = mybir.dt.float32
BF16 = mybir.dt.bfloat16
I32 = mybir.dt.int32
U32 = mybir.dt.uint32
U16 = mybir.dt.uint16
U8 = mybir.dt.uint8
E4M3 = mybir.dt.float8_e4m3fn_x4
E5M2 = mybir.dt.float8_e5m2_x4
E2M1 = mybir.dt.float4_e2m1fn_x4
ALU = mybir.AluOpType
ACT = mybir.ActivationFunctionType
AX = mybir.AxisListType

P = 128
PACK = 4
HALF = 128
BUNDLE = J // G
LINE = 4


def load_scale_rows(queue, plane, first_row, scales, quadrants):
    for q in quadrants:
        row = 32 * q + first_row
        queue.dma_start(out=plane[row : row + 4, :].bitcast(I32), in_=scales[0, 4 * q : 4 * q + 4, :].bitcast(I32))


def tile_list_sum_largerpicks_othertable_levelled_rowshares_kernel(
    tc, xf, fk, w_words, w_scales, xo_words, xo_scales, w2_words, w2_scales, wb_words, wb_scales, bi, offs, offs2, offs3, out
):
    nc = tc.nc
    with ExitStack() as ctx:
        sb = ctx.enter_context(tc.tile_pool(name="sb", bufs=1))
        ps = ctx.enter_context(tc.psum_pool(name="ps", bufs=1))

        list1 = sb.tile([P, J // 16], U16, name="list1")
        list2 = sb.tile([P, J // 16], U16, name="list2")
        list3 = sb.tile([P, J // 16], U16, name="list3")
        x_pair = [sb.tile([P, 2, T], F32, name=f"x_pair{a}", tag=f"x_pair{a}", align_bytes=64) for a in range(2)]
        factor = sb.tile([P, PACK], F32, name="factor")
        xo_w = sb.tile([P, Z], U16, name="xo_w", tag="xo_w", align_bytes=64)
        xo_s = sb.tile([P, Z], U8, name="xo_s", align_bytes=64)
        w_raw = sb.tile([P, R], U32, name="w_raw", align_bytes=64)
        w2_raw = sb.tile([P, R], U32, name="w2_raw", align_bytes=64)
        ws_raw = sb.tile([P, R], U8, name="ws_raw", tag="larger", align_bytes=64)
        wb_s = sb.tile([P, N], U8, name="wb_s", align_bytes=64)

        nc.vector.memset(xo_s[:].bitcast(I32), 0)
        nc.vector.memset(ws_raw[:].bitcast(I32), 0)
        warm = sb.tile([P, 2], F32, name="warm")
        nc.vector.memset(warm[:, 0:1], 0.0)
        nc.scalar.activation(warm[:, 1:2], warm[:, 0:1], ACT.Exp)
        nc.vector.memset(wb_s[:].bitcast(I32), 0)

        def load_words(tile, words):
            nc.sync.dma_start(out=tile.bitcast(I32), in_=words.bitcast(I32))

        x_rows = xf.rearrange("(p t) c -> p t c", t=PACK)
        load_scale_rows(nc.gpsimd, ws_raw, 0, w2_scales, range(1, 4))
        nc.sync.dma_start(list1[:], offs)
        nc.sync.dma_start(list2[:], offs2)
        nc.sync.dma_start(out=x_pair[0][:], in_=x_rows[:, 0:2, :])
        nc.sync.dma_start(list3[:], offs3)
        load_words(xo_w[:], xo_words[0])
        load_scale_rows(nc.sync, xo_s, 0, xo_scales, range(4))
        nc.sync.dma_start(out=x_pair[1][:], in_=x_rows[:, 2:4, :])
        load_words(w2_raw[:], w2_words[0].rearrange("p n t -> p (n t)"))
        load_words(w_raw[:], w_words[0].rearrange("p n t -> p (n t)"))
        load_scale_rows(nc.sync, ws_raw, 4, w_scales, range(4))
        load_scale_rows(nc.sync, ws_raw, 0, w2_scales, range(1))
        nc.sync.dma_start(out=factor[:], in_=fk.rearrange("(p t) o -> p (t o)", t=PACK))
        load_scale_rows(nc.sync, wb_s, 0, wb_scales, range(4))

        halves = range(J // HALF)

        def cols(h):
            return slice(h * HALF, (h + 1) * HALF)

        def entries(h):
            return slice(h * HALF // 16, (h + 1) * HALF // 16)

        pick1 = sb.tile([P, PACK, J], F32, name="pick1")
        pick2 = sb.tile([P, PACK, J], F32, name="pick2")
        nc.vector.tensor_copy(pick2[:, 0, :], x_pair[0][:, 0, :].indirect(list2[:]))
        for e in range(2):
            nc.scalar.activation(pick1[:, e, :], x_pair[0][:, e, :].indirect(list1[:]), ACT.Copy)
        nc.scalar.activation(pick2[:, 1, :], x_pair[0][:, 1, :].indirect(list2[:]), ACT.Copy)
        for h in halves:
            for picked, entry_list in ((pick1, list1), (pick2, list2)):
                for e in range(2):
                    nc.scalar.activation(
                        picked[:, 2 + e, cols(h)], x_pair[1][:, e, :].indirect(entry_list[:, entries(h)]), ACT.Copy
                    )

        wb_w = sb.tile([P, 2 * N], U8, name="wb_w", tag="x_pair0", align_bytes=64)
        load_words(wb_w[:], wb_words[0])

        xg_w = sb.tile([P, J], U16, name="xg_w", align_bytes=64)
        xg_s = sb.tile([P, J], U8, name="xg_s", align_bytes=64)
        nc.vector.tensor_copy(xg_s[:], xo_s[:].indirect(list3[:]))
        nc.vector.tensor_copy(xg_w[:], xo_w[:].indirect(list3[:]))
        bias = sb.tile([P, N], F32, name="bias", tag="xo_w", align_bytes=64)
        nc.sync.dma_start(out=bias[:], in_=bi[0].partition_broadcast(P))

        w_dealt = sb.tile([P, PACK, P], U32, name="w_dealt", align_bytes=64)
        w2_dealt = sb.tile([P, PACK, P], U32, name="w2_dealt", align_bytes=64)
        ws_dealt = sb.tile([P, PACK, P], U8, name="ws_dealt", align_bytes=64)

        def deal_words(dealt, raw):
            nc.vector.tensor_copy(
                dealt.rearrange("p t (c i) -> p c t i", i=LINE),
                raw.rearrange("p (c i t) -> p c t i", i=LINE, t=PACK),
            )

        larger = []

        def keep_larger(h):
            larger.append(sb.tile([P, PACK, HALF], F32, name=f"larger{h}", tag="larger", align_bytes=64))
            nc.vector.tensor_tensor(larger[h][:], pick1[:, :, cols(h)], pick2[:, :, cols(h)], ALU.max)

        deal_words(w2_dealt[:], w2_raw[:])
        deal_words(w_dealt[:], w_raw[:])
        nc.vector.tensor_copy(ws_dealt[:], ws_raw[:].rearrange("p (m t) -> p t m", t=PACK))
        keep_larger(0)

        u_b = [sb.tile([P, HALF, PACK], BF16, name="u_b0", align_bytes=64)]
        u_w = [sb.tile([P, HALF], U32, name=f"u_w{h}", align_bytes=64) for h in halves]
        u_s = [sb.tile([P, HALF], U8, name=f"u_s{h}", align_bytes=64) for h in halves]
        hid_b = [sb.tile([P, HALF, PACK], BF16, name=f"hid_b{h}", align_bytes=64) for h in halves]
        hid_w = [sb.tile([P, HALF], U32, name=f"hid_w{h}", align_bytes=64) for h in halves]
        hid_s = [sb.tile([P, HALF], U8, name=f"hid_s{h}", align_bytes=64) for h in halves]
        sums = []
        means = [sb.tile([P, PACK, HALF // BUNDLE], F32, name=f"means{h}") for h in halves]
        neg_z = [sb.tile([P, N], F32, name=f"neg_z{h}") for h in halves]
        neg_max = [sb.tile([P, 1], F32, name=f"neg_max{h}") for h in halves]
        ea = [sb.tile([P, N], F32, name=f"ea{h}") for h in halves]
        total = [sb.tile([P, 1], F32, name=f"total{h}") for h in halves]
        inv = [sb.tile([P, 1], F32, name=f"inv{h}") for h in halves]
        y = [sb.tile([P, N], F32, name=f"y{h}") for h in halves]
        a_ps = [ps.tile([P, PACK, HALF], F32, name=f"a_ps{h}") for h in halves]
        p_ps = [ps.tile([P, N], F32, name=f"p_ps{h}") for h in halves]

        def scale_u(h):
            nc.vector.tensor_tensor(
                u_b[h][:].rearrange("p (c i) t -> p c t i", i=LINE),
                larger[h][:].rearrange("p t (c i) -> p c t i", i=LINE),
                factor[:].unsqueeze(1).unsqueeze(3).to_broadcast([P, HALF // LINE, PACK, LINE]),
                ALU.mult,
            )

        def quantise(words, scales, values, fmt):
            nc.vector.quantize_mx(out=words[:].bitcast(fmt), scales=scales[:], in_=values[:].rearrange("p j t -> p (j t)"))

        def side_passes(h):
            for t in range(PACK):
                nc.tensor.matmul_mx(
                    out=a_ps[h][:, t, :],
                    lhsT=w2_dealt[:, t, :].bitcast(E5M2),
                    lhsT_scale=ws_dealt[:, t, :],
                    rhs=xg_w[:, cols(h)].bitcast(E2M1),
                    rhs_scale=xg_s[:, cols(h)],
                    start=(t == 0),
                    stop=False,
                )

        def main_passes(h):
            for t in range(PACK):
                nc.tensor.matmul_mx(
                    out=a_ps[h][:, t, :],
                    lhsT=w_dealt[:, t, :].bitcast(E4M3),
                    lhsT_scale=ws_dealt[4:P, t, :],
                    rhs=u_w[h][:].bitcast(E4M3),
                    rhs_scale=u_s[h][:],
                    start=False,
                    stop=(t == PACK - 1),
                )

        def bundle_sums(h, tag):
            sums.append(sb.tile([P, PACK, HALF // BUNDLE], F32, name=f"sums{h}", tag=tag, align_bytes=64))
            nc.vector.tensor_reduce(
                sums[h][:].rearrange("p t g -> p (t g)"),
                a_ps[h][:].rearrange("p t (g i) -> p (t g) i", i=BUNDLE),
                AX.X,
                ALU.add,
            )

        def bundle_means(h):
            nc.scalar.activation(means[h][:], sums[h][:], ACT.Copy, scale=1.0 / BUNDLE)

        def level(h):
            nc.vector.tensor_tensor(
                hid_b[h][:].rearrange("p (g i) t -> p g i t", i=BUNDLE),
                a_ps[h][:].rearrange("p t (g i) -> p g i t", i=BUNDLE),
                means[h][:].rearrange("p t g -> p g t").unsqueeze(2).to_broadcast([P, HALF // BUNDLE, BUNDLE, PACK]),
                ALU.subtract,
            )

        def second_layer(h):
            nc.tensor.matmul_mx(
                out=p_ps[h][:],
                lhsT=hid_w[h][:].bitcast(E5M2),
                lhsT_scale=hid_s[h][:],
                rhs=wb_w[:].bitcast(E2M1),
                rhs_scale=wb_s[:],
                start=True,
                stop=True,
            )

        def logits(h):
            nc.vector.scalar_tensor_tensor(neg_z[h][:], p_ps[h][:], -0.7, bias[:], ALU.mult, ALU.subtract)

        def row_max(h):
            nc.vector.tensor_reduce(neg_max[h][:], neg_z[h][:], AX.X, ALU.min)

        def exponentials(h):
            nc.scalar.activation(ea[h][:], neg_z[h][:], ACT.Exp, bias=neg_max[h][:], scale=-1.0, accum_out=total[h][:])

        def invert(h):
            nc.vector.reciprocal(inv[h][:], total[h][:])

        def shares(h):
            nc.vector.tensor_scalar(y[h][:], ea[h][:], inv[h][:], 256.0, ALU.mult, ALU.mult)
            nc.sync.dma_start(out=out[cols(h), :], in_=y[h][:])

        side_passes(0)
        side_passes(1)
        scale_u(0)
        keep_larger(1)
        quantise(u_w[0], u_s[0], u_b[0], E4M3)
        main_passes(0)
        u_b.append(sb.tile([P, HALF, PACK], BF16, name="u_b1", tag="u_b1", align_bytes=64))
        scale_u(1)
        quantise(u_w[1], u_s[1], u_b[1], E4M3)
        main_passes(1)
        bundle_sums(0, "u_b1")
        bundle_means(0)
        bundle_sums(1, "sums1")
        bundle_means(1)
        for h in halves:
            level(h)
        for h in halves:
            quantise(hid_w[h], hid_s[h], hid_b[h], E5M2)
            second_layer(h)
        for h in halves:
            logits(h)
        for h in halves:
            row_max(h)
            exponentials(h)
        for h in halves:
            invert(h)
            shares(h)
